import numpy as np
import ml_dtypes


def mxq(x, axis, fmt="e4m3"):
    dtype, down = {"e4m3": (ml_dtypes.float8_e4m3fn, 7), "e5m2": (ml_dtypes.float8_e5m2, 14)}[fmt]
    v = np.moveaxis(np.asarray(x, np.float32).astype(ml_dtypes.bfloat16).astype(np.float64), axis, -1)
    blocks = v.reshape(v.shape[:-1] + (-1, 32))
    amax = np.abs(blocks).max(-1, keepdims=True)
    byte = np.maximum(np.where(amax > 0, np.frexp(amax)[1] - 1 + 127, 0) - down, 1)
    scale = np.exp2(byte - 127.0)
    codes = (blocks / scale).astype(np.float32).astype(dtype).astype(np.float64)
    return np.moveaxis((codes * scale).reshape(v.shape), -1, axis)


WIDE = False


def mx_kscale(k):
    if not WIDE:
        return np.ones(k)
    levels = np.array([10, -10, 5, -5, 0])
    if k % 512:
        return np.exp2(np.random.permutation(np.resize(levels, k // 32))).repeat(32)
    a = np.empty((k // 512, 16))
    for p in range(k // 512):
        a[p, :8] = np.random.permutation(np.resize(levels, 8))
        for g in range(8):
            far = levels[np.abs(levels - a[p, g]) >= 10]
            a[p, g + 8] = far[np.random.randint(len(far))]
    return np.exp2(a.ravel()).repeat(32)


BF16 = ml_dtypes.bfloat16


def bf(x):
    return np.asarray(x, np.float32).astype(BF16)


def f64(x):
    return np.asarray(x).astype(np.float64)


E2M1 = np.array([0.0, 0.5, 1.0, 1.5, 2.0, 3.0, 4.0, 6.0, -0.0, -0.5, -1.0, -1.5, -2.0, -3.0, -4.0, -6.0])


def pack_weight(w, fmt):
    k, n = w.shape
    w = f64(bf(w)).reshape(k // 32, 32, n)
    amax = np.abs(w).max(1)
    if fmt == "e4m3":
        byte = np.frexp(amax)[1] - 1 + 127 - 7
    else:
        mant, ex = np.frexp(amax / 6.0)
        byte = np.where(mant > 0.5, ex, ex - 1) + 127
    byte = np.clip(np.where(amax > 0, byte, 1), 1, 254)
    scaled = (w * np.exp2(127.0 - byte)[:, None, :]).reshape(k, n).astype(np.float32)
    by_word = np.ascontiguousarray(scaled.reshape(k // 512, 128, 4, n).transpose(0, 1, 3, 2))
    if fmt == "e4m3":
        words = by_word.astype(ml_dtypes.float8_e4m3fn).view(np.uint8)
    else:
        c = by_word.astype(ml_dtypes.float4_e2m1fn).view(np.uint8) & 0xF
        words = c[..., 0::2] | (c[..., 1::2] << 4)
    return np.ascontiguousarray(words), np.ascontiguousarray(byte.astype(np.uint8).reshape(k // 512, 16, n))


def unpack_weight(words, scales, fmt):
    g, p, n, _ = words.shape
    if fmt == "e4m3":
        vals = np.ascontiguousarray(words).view(ml_dtypes.float8_e4m3fn).astype(np.float64)
    else:
        nib = np.empty((g, p, n, 4), np.uint8)
        nib[..., 0::2] = words & 0xF
        nib[..., 1::2] = words >> 4
        vals = E2M1[nib]
    vals = vals * np.repeat(np.exp2(scales.astype(np.float64) - 127.0), 8, axis=1)[..., None]
    return vals.transpose(0, 1, 3, 2).reshape(g * 512, n)
def pack4(w):
    words, scales = pack_weight(w, "e2m1")
    return words.reshape(words.shape[0], 128, -1), scales


def unpack4(words, scales):
    return unpack_weight(words.reshape(words.shape[0], 128, -1, 2), scales, "e2m1")


def planes(Y):
    n, m = Y.shape
    b = f64(bf(Y)).reshape(n // 32, 32, m)
    amax = np.abs(b).max(1)
    byte = np.clip(np.where(amax > 0, np.frexp(amax)[1] - 1 + 127 - 7, 1), 1, 254)
    codes = (b * np.exp2(127.0 - byte)[:, None, :]).reshape(n, m).astype(np.float32).astype(ml_dtypes.float8_e4m3fn).view(np.uint8)
    words = codes.reshape(n // 512, 128, 4, m).transpose(0, 1, 3, 2)
    return np.ascontiguousarray(words), np.ascontiguousarray(byte.astype(np.uint8).reshape(n // 512, 16, m))


S, LB, LK, RB, RK = 4, 1024, 512, 1024, 1024

def setup_inputs():
    s = mx_kscale(LB)
    t = mx_kscale(S * LK)
    bra = np.random.randn(LB, S * RB) / np.sqrt(LB)
    env = np.random.randn(LB, LK)
    ket = np.random.randn(S * LK, RK) / np.sqrt(S * LK)
    weight = np.exp(0.3 * np.random.randn(S * LK))
    local = 0.5 * np.random.randn(RB, RK)
    row_scale = np.exp(0.8 * np.random.randn(RB))
    bra_words, bra_scales = pack4(bra * s[:, None])
    env_words, env_scales = pack4(env / s[:, None])
    return {"bra_words": bra_words, "bra_scales": bra_scales,
            "env_words": env_words, "env_scales": env_scales,
            "weight": bf((weight * t).reshape(S, LK)),
            "ket": bf(ket / t[:, None]),
            "local": bf(local), "row_scale": bf(row_scale)}

def reference(bra_words, bra_scales, env_words, env_scales, weight, ket, local, row_scale):
    bra = unpack4(bra_words, bra_scales)
    env = unpack4(env_words, env_scales)
    half = (bra.T @ env).reshape(S, RB, LK)
    half = half * f64(weight)[:, None, :]
    fused = half.transpose(1, 0, 2).reshape(RB, S * LK)
    new = mxq(fused, 1, "e4m3") @ mxq(f64(ket), 0, "e4m3")
    y = (new + f64(local)) * f64(row_scale)[:, None]
    Y = y.reshape(RB, RK)
    words, scales = planes(Y)
    return y, words, scales

@@ -1,0 +1,321 @@
+from contextlib import ExitStack
+
+import concourse.mybir as mybir
+
+S, LB, LK, RB, RK = 4, 1024, 512, 1024, 1024
+FLOPS = 2 * LB * S * RB * LK + 2 * RB * S * LK * RK
+
+F32 = mybir.dt.float32
+BF16 = mybir.dt.bfloat16
+I32 = mybir.dt.int32
+U32 = mybir.dt.uint32
+U8 = mybir.dt.uint8
+FP8X4 = mybir.dt.float8_e4m3fn_x4
+FP4X4 = mybir.dt.float4_e2m1fn_x4
+ALU = mybir.AluOpType
+COPY = mybir.ActivationFunctionType.Copy
+
+P = 128
+PACK = 4
+KP = 512
+BANK = 512
+WIDE = 5
+
+FIRST_ORDER = [(0, 0), (1, 0), (0, 1), (1, 1), (0, 2), (0, 3), (1, 2), (1, 3)]
+OUT_UNITS = [(0, 0, 512), (1, 0, 512), (0, 512, 512), (1, 512, 256), (1, 768, 256)]
+ORDER = {
+    "T": "S1_00 S1_10 S1_01 S1_11 S1_02 S1_03 S1_12 S1_13 p0 p1 b2 b3 b4",
+    "S": "w32 E1_00 E1_10 E1_01 E1_11 rs32 E1_02 E1_03 E1_12 E1_13 LRS_0 KI21 LRS_1 KI31 YI0 LRSh20 YI1 LRS_3 YI2 YI3",
+    "V": "Z env0 env1 env2 env3 KI00 KQ00 FI00 KI01 FQ00 FI10 KQ01 KI10 FQ10 FI01 KQ10 KI11 FQ01 FI11 KQ11 KI20 FQ11 FI02 KQ20 KI30 FQ02 FI03 KQ30 FI12 FQ03 FI13 FQ12 E2h00 FQ13 E2h01 KQ21 E2h10 KQ31 E2h11 LRSh21 YQ0 E2_2 LRS_4 YQ1 E2_3 YQ2 E2_4 YQ3 YI4 YQ4",
+    "D": "le les lbs0 lb00 lw lk00 lb10 lbs1 lb1 lk01 lk1 lbs2 lb2 lrs lbs3 lb3 lk2 lk3 ll0 ll1 sy0 sy1 sc00 sy2 sc10 sy3 sc01 ss0 sy4 sc11 ss1",
+}
+
+
+def tile_site_environment_absorption_k5_kernel(
+    tc, bra_words, bra_scales, env_words, env_scales, weight, ket, local, row_scale, out_0, out_1, out_2
+):
+    nc = tc.nc
+    with ExitStack() as ctx:
+        sb = ctx.enter_context(tc.tile_pool(name="sb", bufs=1))
+        psum = ctx.enter_context(tc.psum_pool(name="psum", bufs=1))
+        ctx.enter_context(tc.manual_schedule())
+
+        def keep(name, shape, dtype):
+            return sb.tile(shape, dtype, name=name, align_bytes=64)
+
+        env_raw = keep("env_raw", [P, 2, 2 * LK], U8)
+        env_sraw = keep("env_sraw", [P, 2, LK], U8)
+        env_w = [keep("env_w%d" % t, [P, 2, 2 * P], U8) for t in range(PACK)]
+        env_s = [keep("env_s%d" % t, [P, 2, P], U8) for t in range(PACK)]
+        bra_w = {gu: keep("bra_w%d%d" % gu, [P, 2, 2 * BANK], U8) for gu in FIRST_ORDER[:2]}
+        bra_wu = {u: keep("bra_wu%d" % u, [P, 2, 2 * RB], U8) for u in range(1, S)}
+        bra_s = [keep("bra_s%d" % u, [P, 2, RB], U8) for u in range(S)]
+        w_raw = keep("w_raw", [P, S, PACK], BF16)
+        w32 = keep("w32", [P, S * PACK], F32)
+        rs_raw = keep("rs_raw", [P, 2, PACK], BF16)
+        rs32 = keep("rs32", [P, 2 * PACK], F32)
+        ket_first = [keep("ket_first%d" % jh, [P, PACK, BANK], BF16) for jh in range(2)]
+        ket_rest = {u: keep("ket_rest%d" % u, [P, PACK, RK], BF16) for u in range(1, S)}
+        halves = [(u, jh) for u in range(S) for jh in range(2)]
+        ket_c = {k: keep("ket_c%d%d" % k, [P, BANK], U32) for k in halves}
+        ket_s = {k: keep("ket_s%d%d" % k, [P, BANK], U8) for k in halves}
+        f_raw = {gu: keep("f_raw%d%d" % gu, [P, PACK, KP], BF16) for gu in FIRST_ORDER}
+        f_c = {gu: keep("f_c%d%d" % gu, [P, KP], U32) for gu in FIRST_ORDER}
+        f_s = {gu: keep("f_s%d%d" % gu, [P, KP], U8) for gu in FIRST_ORDER}
+        loc = [keep("loc%d" % g, [P, PACK, RK], BF16) for g in range(2)]
+        y32 = [keep("y32_%d" % n, [P, PACK, w], F32) for n, (g, j0, w) in enumerate(OUT_UNITS)]
+        y_c = {(g, jh): keep("y_c%d%d" % (g, jh), [P, BANK], U32) for g in range(2) for jh in range(2)}
+        y_s = [keep("y_s%d" % g, [P, RK], U8) for g in range(2)]
+
+        queue = {"D": nc.sync, "G": nc.gpsimd, "S": nc.scalar}
+        jobs = {}
+        live = {}
+
+        def job(name, needs, run, slot=None, frees=None):
+            jobs[name] = (needs, run, slot, frees)
+
+        def fresh(tag, pool, shape, dtype, key):
+            if pool is psum:
+                live[key] = pool.tile(shape, dtype, name=tag)
+            else:
+                live[key] = pool.tile(shape, dtype, name=tag, align_bytes=64)
+            return live[key]
+
+        def interleave(engine, dst, src):
+            d = dst.rearrange("p (c i t) -> p c t i", i=4, t=PACK)
+            s = src.rearrange("p t (c i) -> p c t i", i=4)
+            if engine == "V":
+                nc.vector.tensor_copy(out=d, in_=s)
+            else:
+                nc.scalar.copy(out=d, in_=s)
+
+        pe_units = ORDER["T"].split()
+        on_gpsimd = "LRS" in ORDER.get("G", "")
+
+        def load(name, dst, src, needs=()):
+            job(name, list(needs), lambda e: queue[e].dma_start(out=dst, in_=src))
+
+        def load_scales(name, plane, src, cols):
+            job(("zero", name), [], lambda e: nc.vector.memset(plane[:].bitcast(I32), 0))
+            for q in range(4):
+                load(("ld", name, q), plane[32 * q : 32 * q + 4].bitcast(I32),
+                     src[:, 4 * q : 4 * q + 4, cols].rearrange("h r n -> r h n").bitcast(I32), [("zero", name)])
+
+        load(("ld", "env"), env_raw[:].bitcast(I32), env_words.rearrange("h p n -> p h n").bitcast(I32))
+        load_scales("env_s", env_sraw, env_scales, slice(0, LK))
+        for u in range(S):
+            load_scales("bra_s%d" % u, bra_s[u], bra_scales, slice(RB * u, RB * (u + 1)))
+        bra_view = bra_words.rearrange("h p n -> p h n")
+        for g in range(2):
+            load(("ld", "bra", g, 0), bra_w[(g, 0)][:].bitcast(I32), bra_view[:, :, 2 * BANK * g : 2 * BANK * (g + 1)].bitcast(I32))
+        for u in range(1, S):
+            load(("ld", "brau", u), bra_wu[u][:].bitcast(I32), bra_view[:, :, 2 * RB * u : 2 * RB * (u + 1)].bitcast(I32))
+        load(("ld", "w"), w_raw[:], weight.rearrange("u (p t) -> p u t", t=PACK))
+        load(("ld", "rs"), rs_raw[:], row_scale.rearrange("(g p t) -> p g t", g=2, t=PACK))
+        for jh in range(2):
+            load(("ld", "ket", 0, jh), ket_first[jh][:],
+                 ket[0:KP, BANK * jh : BANK * (jh + 1)].rearrange("(p t) j -> p t j", t=PACK))
+        for u in range(1, S):
+            load(("ld", "ket", u), ket_rest[u][:], ket[KP * u : KP * (u + 1), :].rearrange("(p t) j -> p t j", t=PACK))
+        for g in range(2):
+            load(("ld", "loc", g), loc[g][:], local[KP * g : KP * (g + 1), :].rearrange("(p t) j -> p t j", t=PACK))
+
+        job(("w32",), [("ld", "w")],
+            lambda e: nc.scalar.activation(out=w32[:], in_=w_raw[:].rearrange("p u t -> p (u t)"), func=COPY))
+        job(("rs32",), [("ld", "rs")],
+            lambda e: nc.scalar.activation(out=rs32[:], in_=rs_raw[:].rearrange("p g t -> p (g t)"), func=COPY))
+
+        def env_perm(t):
+            job(("envw", t), [("ld", "env")], lambda e: nc.vector.tensor_copy(
+                out=env_w[t][:].rearrange("p h (m b) -> p h m b", b=2),
+                in_=env_raw[:].rearrange("p h (m t b) -> p t h m b", t=PACK, b=2)[:, t]))
+            job(("envs", t), [("ld", "env_s", q) for q in range(4)], lambda e: nc.vector.tensor_copy(
+                out=env_s[t][:], in_=env_sraw[:].rearrange("p h (m t) -> p t h m", t=PACK)[:, t]))
+
+        for t in range(PACK):
+            env_perm(t)
+
+        def first(g, u, t):
+            bank = PACK * (pe_units.index("S1_%d%d" % (g, u)) % 2) + t
+            if u == 0:
+                words, wcols, wload = bra_w[(g, u)], slice(0, 2 * BANK), ("ld", "bra", g, 0)
+            else:
+                words, wcols, wload = bra_wu[u], slice(2 * BANK * g, 2 * BANK * (g + 1)), ("ld", "brau", u)
+            plane, s0, sname = bra_s[u], BANK * g, "bra_s%d" % u
+
+            def mm(e):
+                acc = fresh("bank%d" % bank, psum, [P, BANK], F32, ("H", g, u, t))
+                for h in range(2):
+                    nc.tensor.matmul_mx(
+                        out=acc[:], lhsT=env_w[t][:, h, :].bitcast(FP4X4), lhsT_scale=env_s[t][:, h, :],
+                        rhs=words[:, h, wcols].bitcast(FP4X4), rhs_scale=plane[:, h, s0 : s0 + BANK],
+                        start=(h == 0), stop=(h == 1))
+
+            job(("S1", g, u, t), [("envw", t), ("envs", t), wload] + [("ld", sname, q) for q in range(4)], mm,
+                slot="bank%d" % bank)
+            job(("E1", g, u, t), [("S1", g, u, t), ("w32",)], lambda e: nc.scalar.activation(
+                out=f_raw[(g, u)][:, t, :].rearrange("p (s m) -> p s m", s=PACK),
+                in_=live[("H", g, u, t)][:].rearrange("p (m s) -> p s m", s=PACK),
+                func=COPY, scale=w32[:, PACK * u + t : PACK * u + t + 1]), frees="bank%d" % bank)
+
+        for (g, u) in FIRST_ORDER:
+            for t in range(PACK):
+                first(g, u, t)
+
+        def quant(kind, key, needs, src, width, codes, scales, slot):
+            tag = "wide%d" % slot
+            job((kind + "I",) + key, needs,
+                lambda e: interleave(e, fresh(tag, sb, [P, PACK * width], BF16, (kind,) + key)[:], src), slot=tag)
+            job((kind + "Q",) + key, [(kind + "I",) + key], lambda e: nc.vector.quantize_mx(
+                out=codes.bitcast(FP8X4), scales=scales, in_=live[(kind,) + key][:]), frees=tag)
+
+        def second(n, g, j0, w, s):
+            bank = PACK * ([w[1:] for w in pe_units].index(str(n)) % 2) + s
+            jh, c0 = divmod(j0, BANK)
+
+            def mm(u):
+                def run(e):
+                    if u == 0:
+                        fresh("bank%d" % bank, psum, [P, BANK], F32, ("Z", n, s))
+                    nc.tensor.matmul_mx(
+                        out=live[("Z", n, s)][:, 0:w],
+                        lhsT=f_c[(g, u)][:, P * s : P * (s + 1)].bitcast(FP8X4),
+                        lhsT_scale=f_s[(g, u)][:, P * s : P * (s + 1)],
+                        rhs=ket_c[(u, jh)][:, c0 : c0 + w].bitcast(FP8X4), rhs_scale=ket_s[(u, jh)][:, c0 : c0 + w],
+                        start=(u == 0), stop=(u == S - 1))
+                return run
+
+            for u in range(S):
+                job(("S2", n, s, u), [("FQ", g, u), ("KQ", u, jh)] + ([("S2", n, s, u - 1)] if u else []), mm(u),
+                    slot="bank%d" % bank if u == 0 else None)
+            col = rs32[:, PACK * g + s : PACK * g + s + 1]
+            tag = "lrs%d" % (s if on_gpsimd else PACK * (n % 2) + s)
+
+            def lrs(e):
+                dst = fresh(tag, sb, [P, w], F32, ("L", n, s))
+                if e == "S":
+                    nc.scalar.activation(out=dst[:], in_=loc[g][:, s, j0 : j0 + w], func=COPY, scale=col)
+                elif e == "G":
+                    nc.gpsimd.tensor_scalar(out=dst[:], in0=loc[g][:, s, j0 : j0 + w], scalar1=col, scalar2=0.0,
+                                            op0=ALU.mult, op1=ALU.add)
+                else:
+                    nc.vector.tensor_scalar(out=dst[:], in0=loc[g][:, s, j0 : j0 + w], scalar1=col, scalar2=None, op0=ALU.mult)
+
+            job(("LRS", n, s), [("ld", "loc", g), ("rs32",)] + ([("E2", n - 1, s)] if on_gpsimd and n else []), lrs, slot=tag)
+            job(("E2", n, s), [("S2", n, s, S - 1), ("LRS", n, s)], lambda e: nc.vector.scalar_tensor_tensor(
+                out=y32[n][:, s, :], in0=live[("Z", n, s)][:, 0:w], scalar=col, in1=live[("L", n, s)][:],
+                op0=ALU.mult, op1=ALU.add), frees=("bank%d" % bank, tag))
+
+        for n, (g, j0, w) in enumerate(OUT_UNITS):
+            for s in range(PACK):
+                second(n, g, j0, w, s)
+
+        def store_rows(n, g, j0, w, s0, ns):
+            rows = out_0[KP * g : KP * (g + 1), j0 : j0 + w].rearrange("(p t) j -> p t j", t=PACK)
+            job(("st", "y", n, s0), [("E2", n, s) for s in range(s0, s0 + ns)], lambda e: queue[e].dma_start(
+                out=rows[:, s0 : s0 + ns, :], in_=y32[n][:, s0 : s0 + ns, :]))
+
+        def store_codes(g, jh):
+            job(("st", "c", g, jh), [("YQ", n) for n, x in enumerate(OUT_UNITS) if x[0] == g and x[1] // BANK == jh],
+                lambda e: queue[e].dma_start(
+                    out=out_1[g, :, BANK * jh : BANK * (jh + 1), :].rearrange("p m t -> p (m t)").bitcast(I32),
+                    in_=y_c[(g, jh)][:].bitcast(I32)))
+
+        def store_scales(g, q):
+            job(("st", "s", g, q), [("YQ", n) for n, x in enumerate(OUT_UNITS) if x[0] == g],
+                lambda e: queue[e].dma_start(out=out_2[g, 4 * q : 4 * q + 4, :].bitcast(I32),
+                                             in_=y_s[g][32 * q : 32 * q + 4, :].bitcast(I32)))
+
+        for n, (g, j0, w) in enumerate(OUT_UNITS):
+            for s0 in (0, 2):
+                store_rows(n, g, j0, w, s0, 2)
+        for g in range(2):
+            for q in range(4):
+                store_scales(g, q)
+            for jh in range(2):
+                store_codes(g, jh)
+
+        def unit(kind, *key):
+            return [(kind,) + key + (s,) for s in range(PACK)]
+
+        def expand(word):
+            d = tuple(int(c) for c in word.split("_")[-1] if c in "0123456789")
+            kind = "".join(c for c in word if c not in "0123456789")
+            if word[:2] in ("S1", "E1", "E2"):
+                d = tuple(int(c) for c in word[3:])
+                kind = word[:3]
+            if kind == "b":
+                return [("S2", d[0], s, u) for s in range(PACK) for u in range(S)]
+            if kind == "p":
+                return [("S2", d[0], s, u) for u in range(S) for s in range(PACK)]
+            if kind in ("S1_", "E1_", "E2_", "LRS_"):
+                return unit(kind[:-1], *d)
+            if kind in ("E2h", "LRSh"):
+                return [(kind[:-1], d[0], 2 * d[1]), (kind[:-1], d[0], 2 * d[1] + 1)]
+            if kind == "env":
+                return [("envw", d[0]), ("envs", d[0])]
+            if word in ("w32", "rs32"):
+                return [(word,)]
+            if word == "Z":
+                return [("zero", "env_s")] + [("zero", "bra_s%d" % u) for u in range(S)]
+            if word == "le":
+                return [("ld", "env")]
+            if word == "les":
+                return unit("ld", "env_s")
+            if kind == "lbs":
+                return unit("ld", "bra_s%d" % d[0])
+            if word in ("lw", "lrs"):
+                return [("ld", word[1:])]
+            if kind == "lb":
+                return [("ld", "bra") + d] if len(d) == 2 else [("ld", "brau") + d]
+            if kind == "lk":
+                return [("ld", "ket") + d]
+            if kind == "ll":
+                return [("ld", "loc") + d]
+            if kind == "sy":
+                return [("st", "y", d[0], 0), ("st", "y", d[0], 2)]
+            if kind == "sc":
+                return [("st", "c") + d]
+            if kind == "ss":
+                return unit("st", "s", *d)
+            return [(kind,) + d]
+
+        order = {e: [j for word in ORDER[e].split() for j in expand(word)] for e in ORDER}
+
+        quantised = [j for j in order["V"] if j[0] in ("KQ", "FQ", "YQ")]
+        for n, j in enumerate(quantised):
+            key = j[1:]
+            if j[0] == "KQ":
+                u, jh = key
+                if u == 0:
+                    need, src = ("ld", "ket", 0, jh), ket_first[jh][:]
+                else:
+                    need, src = ("ld", "ket", u), ket_rest[u][:, :, BANK * jh : BANK * (jh + 1)]
+                quant("K", key, [need], src, BANK, ket_c[key][:], ket_s[key][:], n % WIDE)
+            elif j[0] == "FQ":
+                quant("F", key, unit("E1", *key), f_raw[key][:], KP, f_c[key][:], f_s[key][:], n % WIDE)
+            else:
+                g, j0, w = OUT_UNITS[key[0]]
+                jh, c0 = divmod(j0, BANK)
+                quant("Y", key, unit("E2", *key), y32[key[0]][:], w, y_c[(g, jh)][:, c0 : c0 + w],
+                      y_s[g][:, j0 : j0 + w], n % WIDE)
+
+        assert sorted(map(str, jobs)) == sorted(str(j) for e in order for j in order[e])
+        done = set()
+        taken = set()
+        at = {e: 0 for e in order}
+        for sweep in range(len(jobs)):
+            for e in order:
+                if at[e] < len(order[e]):
+                    name = order[e][at[e]]
+                    needs, run, slot, frees = jobs[name]
+                    if all(d in done for d in needs) and slot not in taken:
+                        run(e)
+                        done.add(name)
+                        at[e] += 1
+                        if slot is not None:
+                            taken.add(slot)
+                        if frees is not None:
+                            for f in (frees if isinstance(frees, tuple) else (frees,)):
+                                taken.remove(f)
+        assert len(done) == len(jobs)

@@ -17,18 +17,15 @@ COPY = mybir.ActivationFunctionType.Copy
 
 P = 128
 PACK = 4
-KP = 512
-BANK = 512
-WIDE = 5
-
-FIRST_ORDER = [(0, 0), (1, 0), (0, 1), (1, 1), (0, 2), (0, 3), (1, 2), (1, 3)]
-OUT_UNITS = [(0, 0, 512), (1, 0, 512), (0, 512, 512), (1, 512, 256), (1, 768, 256)]
-ORDER = {
-    "T": "S1_00 S1_10 S1_01 S1_11 S1_02 S1_03 S1_12 S1_13 p0 p1 b2 b3 b4",
-    "S": "w32 E1_00 E1_10 E1_01 E1_11 rs32 E1_02 E1_03 E1_12 E1_13 LRS_0 KI21 LRS_1 KI31 YI0 LRSh20 YI1 LRS_3 YI2 YI3",
-    "V": "Z env0 env1 env2 env3 KI00 KQ00 FI00 KI01 FQ00 FI10 KQ01 KI10 FQ10 FI01 KQ10 KI11 FQ01 FI11 KQ11 KI20 FQ11 FI02 KQ20 KI30 FQ02 FI03 KQ30 FI12 FQ03 FI13 FQ12 E2h00 FQ13 E2h01 KQ21 E2h10 KQ31 E2h11 LRSh21 YQ0 E2_2 LRS_4 YQ1 E2_3 YQ2 E2_4 YQ3 YI4 YQ4",
-    "D": "le les lbs0 lb00 lw lk00 lb10 lbs1 lb1 lk01 lk1 lbs2 lb2 lrs lbs3 lb3 lk2 lk3 ll0 ll1 sy0 sy1 sc00 sy2 sc10 sy3 sc01 ss0 sy4 sc11 ss1",
-}
+GROUP = P * PACK
+PASSES = LB // GROUP
+HALVES = 2
+RUN = 4
+BRA_PIECES = [(0, GROUP), (GROUP, GROUP), (RB, RB), (2 * RB, RB), (3 * RB, RB)]
+BRA_PLANE_PIECES = [(0, RB), (RB, RB), (2 * RB, 2 * RB)]
+KET_PIECES = {0: [(0, GROUP), (GROUP, GROUP)], 1: [(0, RK)], 2: [(0, RK)], 3: [(0, RK)]}
+STAGING = 6
+WARM_PASSES = 30
 
 
 def tile_site_environment_absorption_k5_kernel(
@@ -36,286 +33,333 @@ def tile_site_environment_absorption_k5_kernel(
 ):
     nc = tc.nc
     with ExitStack() as ctx:
-        sb = ctx.enter_context(tc.tile_pool(name="sb", bufs=1))
+        sbuf = ctx.enter_context(tc.tile_pool(name="sbuf", bufs=1))
         psum = ctx.enter_context(tc.psum_pool(name="psum", bufs=1))
         ctx.enter_context(tc.manual_schedule())
 
         def keep(name, shape, dtype):
-            return sb.tile(shape, dtype, name=name, align_bytes=64)
+            return sbuf.tile(shape, dtype, name=name, align_bytes=64)
 
-        env_raw = keep("env_raw", [P, 2, 2 * LK], U8)
-        env_sraw = keep("env_sraw", [P, 2, LK], U8)
-        env_w = [keep("env_w%d" % t, [P, 2, 2 * P], U8) for t in range(PACK)]
-        env_s = [keep("env_s%d" % t, [P, 2, P], U8) for t in range(PACK)]
-        bra_w = {gu: keep("bra_w%d%d" % gu, [P, 2, 2 * BANK], U8) for gu in FIRST_ORDER[:2]}
-        bra_wu = {u: keep("bra_wu%d" % u, [P, 2, 2 * RB], U8) for u in range(1, S)}
-        bra_s = [keep("bra_s%d" % u, [P, 2, RB], U8) for u in range(S)]
-        w_raw = keep("w_raw", [P, S, PACK], BF16)
-        w32 = keep("w32", [P, S * PACK], F32)
-        rs_raw = keep("rs_raw", [P, 2, PACK], BF16)
-        rs32 = keep("rs32", [P, 2 * PACK], F32)
-        ket_first = [keep("ket_first%d" % jh, [P, PACK, BANK], BF16) for jh in range(2)]
-        ket_rest = {u: keep("ket_rest%d" % u, [P, PACK, RK], BF16) for u in range(1, S)}
-        halves = [(u, jh) for u in range(S) for jh in range(2)]
-        ket_c = {k: keep("ket_c%d%d" % k, [P, BANK], U32) for k in halves}
-        ket_s = {k: keep("ket_s%d%d" % k, [P, BANK], U8) for k in halves}
-        f_raw = {gu: keep("f_raw%d%d" % gu, [P, PACK, KP], BF16) for gu in FIRST_ORDER}
-        f_c = {gu: keep("f_c%d%d" % gu, [P, KP], U32) for gu in FIRST_ORDER}
-        f_s = {gu: keep("f_s%d%d" % gu, [P, KP], U8) for gu in FIRST_ORDER}
-        loc = [keep("loc%d" % g, [P, PACK, RK], BF16) for g in range(2)]
-        y32 = [keep("y32_%d" % n, [P, PACK, w], F32) for n, (g, j0, w) in enumerate(OUT_UNITS)]
-        y_c = {(g, jh): keep("y_c%d%d" % (g, jh), [P, BANK], U32) for g in range(2) for jh in range(2)}
-        y_s = [keep("y_s%d" % g, [P, RK], U8) for g in range(2)]
+        sites = [(g, u) for g in range(HALVES) for u in range(S)]
+        kets = [(u, c) for u in range(S) for c in range(HALVES)]
+        blocks = [(g, c) for g in range(HALVES) for c in range(HALVES)]
 
-        queue = {"D": nc.sync, "G": nc.gpsimd, "S": nc.scalar}
-        jobs = {}
-        live = {}
+        env_raw = keep("env_raw", [P, PASSES, 2 * LK], U8)
+        env_raw_plane = keep("env_raw_plane", [P, PASSES, LK], U8)
+        env_slice = [keep("env_slice%d" % t, [P, PASSES, 2 * P], U8) for t in range(PACK)]
+        env_slice_plane = [keep("env_slice_plane%d" % t, [P, PASSES, P], U8) for t in range(PACK)]
+        bra = {first: keep("bra%d" % first, [P, PASSES, 2 * cols], U8) for first, cols in BRA_PIECES}
+        bra_plane = {first: keep("bra_plane%d" % first, [P, PASSES, cols], U8) for first, cols in BRA_PLANE_PIECES}
+        weight_raw = keep("weight_raw", [P, S * PACK], BF16)
+        weight_col = keep("weight_col", [P, S * PACK], F32)
+        scale_raw = keep("scale_raw", [P, HALVES * PACK], BF16)
+        scale_col = keep("scale_col", [P, HALVES * PACK], F32)
+        ket_rows = {
+            u: {first: keep("ket_rows%d_%d" % (u, first), [P, PACK, cols], BF16) for first, cols in KET_PIECES[u]}
+            for u in range(S)
+        }
+        local_rows = [keep("local_rows%d" % g, [P, PACK, RK], BF16) for g in range(HALVES)]
+        f_rows = {site: keep("f_rows%d%d" % site, [P, PACK, GROUP], BF16) for site in sites}
+        y_rows = {block: keep("y_rows%d%d" % block, [P, PACK, GROUP], F32) for block in blocks}
+        ket_codes = {k: keep("ket_codes%d%d" % k, [P, GROUP], U32) for k in kets}
+        ket_plane = {k: keep("ket_plane%d%d" % k, [P, GROUP], U8) for k in kets}
+        f_codes = {site: keep("f_codes%d%d" % site, [P, GROUP], U32) for site in sites}
+        f_plane = {site: keep("f_plane%d%d" % site, [P, GROUP], U8) for site in sites}
+        y_codes = {block: keep("y_codes%d%d" % block, [P, GROUP], U32) for block in blocks}
+        y_plane = keep("y_plane", [P, HALVES, RK], U8)
 
-        def job(name, needs, run, slot=None, frees=None):
-            jobs[name] = (needs, run, slot, frees)
+        banks = {}
+        staged = {}
 
-        def fresh(tag, pool, shape, dtype, key):
-            if pool is psum:
-                live[key] = pool.tile(shape, dtype, name=tag)
-            else:
-                live[key] = pool.tile(shape, dtype, name=tag, align_bytes=64)
-            return live[key]
+        def group(n):
+            return slice(GROUP * n, GROUP * (n + 1))
 
-        def interleave(engine, dst, src):
-            d = dst.rearrange("p (c i t) -> p c t i", i=4, t=PACK)
-            s = src.rearrange("p t (c i) -> p c t i", i=4)
-            if engine == "V":
-                nc.vector.tensor_copy(out=d, in_=s)
-            else:
-                nc.scalar.copy(out=d, in_=s)
+        def by_slot(rows):
+            return rows.rearrange("(p t) j -> p t j", t=PACK)
 
-        pe_units = ORDER["T"].split()
-        on_gpsimd = "LRS" in ORDER.get("G", "")
+        def window(pieces, first, bytes_a_column=1):
+            start = max(n for n in pieces if n <= first)
+            return pieces[start][:, :, bytes_a_column * (first - start) : bytes_a_column * (first - start + GROUP)]
 
-        def load(name, dst, src, needs=()):
-            job(name, list(needs), lambda e: queue[e].dma_start(out=dst, in_=src))
+        def load(dst, src):
+            nc.sync.dma_start(out=dst, in_=src)
 
-        def load_scales(name, plane, src, cols):
-            job(("zero", name), [], lambda e: nc.vector.memset(plane[:].bitcast(I32), 0))
+        def load_words(dst, words, first, cols):
+            src = words.rearrange("h p n -> p h n")[:, :, 2 * first : 2 * (first + cols)]
+            load(dst[:].bitcast(I32), src.bitcast(I32))
+
+        def load_plane(plane, scales, first, cols):
             for q in range(4):
-                load(("ld", name, q), plane[32 * q : 32 * q + 4].bitcast(I32),
-                     src[:, 4 * q : 4 * q + 4, cols].rearrange("h r n -> r h n").bitcast(I32), [("zero", name)])
+                rows = scales[:, 4 * q : 4 * q + 4, first : first + cols].rearrange("h r n -> r h n")
+                load(plane[32 * q : 32 * q + 4].bitcast(I32), rows.bitcast(I32))
 
-        load(("ld", "env"), env_raw[:].bitcast(I32), env_words.rearrange("h p n -> p h n").bitcast(I32))
-        load_scales("env_s", env_sraw, env_scales, slice(0, LK))
-        for u in range(S):
-            load_scales("bra_s%d" % u, bra_s[u], bra_scales, slice(RB * u, RB * (u + 1)))
-        bra_view = bra_words.rearrange("h p n -> p h n")
-        for g in range(2):
-            load(("ld", "bra", g, 0), bra_w[(g, 0)][:].bitcast(I32), bra_view[:, :, 2 * BANK * g : 2 * BANK * (g + 1)].bitcast(I32))
-        for u in range(1, S):
-            load(("ld", "brau", u), bra_wu[u][:].bitcast(I32), bra_view[:, :, 2 * RB * u : 2 * RB * (u + 1)].bitcast(I32))
-        load(("ld", "w"), w_raw[:], weight.rearrange("u (p t) -> p u t", t=PACK))
-        load(("ld", "rs"), rs_raw[:], row_scale.rearrange("(g p t) -> p g t", g=2, t=PACK))
-        for jh in range(2):
-            load(("ld", "ket", 0, jh), ket_first[jh][:],
-                 ket[0:KP, BANK * jh : BANK * (jh + 1)].rearrange("(p t) j -> p t j", t=PACK))
-        for u in range(1, S):
-            load(("ld", "ket", u), ket_rest[u][:], ket[KP * u : KP * (u + 1), :].rearrange("(p t) j -> p t j", t=PACK))
-        for g in range(2):
-            load(("ld", "loc", g), loc[g][:], local[KP * g : KP * (g + 1), :].rearrange("(p t) j -> p t j", t=PACK))
+        def zero_plane(plane):
+            nc.vector.memset(plane[:].bitcast(I32), 0)
 
-        job(("w32",), [("ld", "w")],
-            lambda e: nc.scalar.activation(out=w32[:], in_=w_raw[:].rearrange("p u t -> p (u t)"), func=COPY))
-        job(("rs32",), [("ld", "rs")],
-            lambda e: nc.scalar.activation(out=rs32[:], in_=rs_raw[:].rearrange("p g t -> p (g t)"), func=COPY))
+        def load_bra(n):
+            first, cols = BRA_PIECES[n]
+            load_words(bra[first], bra_words, first, cols)
 
-        def env_perm(t):
-            job(("envw", t), [("ld", "env")], lambda e: nc.vector.tensor_copy(
-                out=env_w[t][:].rearrange("p h (m b) -> p h m b", b=2),
-                in_=env_raw[:].rearrange("p h (m t b) -> p t h m b", t=PACK, b=2)[:, t]))
-            job(("envs", t), [("ld", "env_s", q) for q in range(4)], lambda e: nc.vector.tensor_copy(
-                out=env_s[t][:], in_=env_sraw[:].rearrange("p h (m t) -> p t h m", t=PACK)[:, t]))
+        def load_bra_plane(n):
+            first, cols = BRA_PLANE_PIECES[n]
+            load_plane(bra_plane[first], bra_scales, first, cols)
+
+        def load_ket(u, n):
+            first, cols = KET_PIECES[u][n]
+            load(ket_rows[u][first][:], by_slot(ket[group(u), first : first + cols]))
+
+        def slice_env(t):
+            nc.vector.tensor_copy(
+                out=env_slice[t][:].rearrange("p h (m b) -> p h m b", b=2),
+                in_=env_raw[:].rearrange("p h (m t b) -> p t h m b", t=PACK, b=2)[:, t],
+            )
+            nc.vector.tensor_copy(
+                out=env_slice_plane[t][:], in_=env_raw_plane[:].rearrange("p h (m t) -> p t h m", t=PACK)[:, t]
+            )
+
+        def take_banks(product):
+            first = PACK * (len(banks) % 2)
+            banks[product] = [psum.tile([P, GROUP], F32, name="bank%d" % (first + t)) for t in range(PACK)]
+            return banks[product]
+
+        def first_product(g, u):
+            acc = take_banks(("h", g, u))
+            words = window(bra, RB * u + GROUP * g, bytes_a_column=2)
+            plane = window(bra_plane, RB * u + GROUP * g)
+            for t in range(PACK):
+                for h in range(PASSES):
+                    nc.tensor.matmul_mx(
+                        out=acc[t][:],
+                        lhsT=env_slice[t][:, h, :].bitcast(FP4X4),
+                        lhsT_scale=env_slice_plane[t][:, h, :],
+                        rhs=words[:, h, :].bitcast(FP4X4),
+                        rhs_scale=plane[:, h, :],
+                        start=(h == 0),
+                        stop=(h == PASSES - 1),
+                    )
+
+        def weigh(g, u):
+            for t in range(PACK):
+                nc.scalar.activation(
+                    out=f_rows[(g, u)][:, t, :].rearrange("p (s m) -> p s m", s=PACK),
+                    in_=banks[("h", g, u)][t][:].rearrange("p (m s) -> p s m", s=PACK),
+                    func=COPY,
+                    scale=weight_col[:, PACK * u + t : PACK * u + t + 1],
+                )
+
+        def interleave(copy, operand, rows):
+            tile = keep("staging%d" % (len(staged) % STAGING), [P, PACK * GROUP], BF16)
+            staged[operand] = tile
+            copy(
+                out=tile[:].rearrange("p (n i t) -> p n t i", i=RUN, t=PACK),
+                in_=rows.rearrange("p t (n i) -> p n t i", i=RUN),
+            )
+
+        def quantise(operand, codes, plane):
+            nc.vector.quantize_mx(out=codes.bitcast(FP8X4), scales=plane, in_=staged[operand][:])
+
+        def mix_ket(copy, u, c):
+            interleave(copy, ("ket", u, c), window(ket_rows[u], GROUP * c))
+
+        def quantise_ket(u, c):
+            quantise(("ket", u, c), ket_codes[(u, c)][:], ket_plane[(u, c)][:])
+
+        def mix_f(copy, g, u):
+            interleave(copy, ("f", g, u), f_rows[(g, u)][:])
+
+        def quantise_f(g, u):
+            quantise(("f", g, u), f_codes[(g, u)][:], f_plane[(g, u)][:])
+
+        def mix_y(copy, g, c):
+            interleave(copy, ("y", g, c), y_rows[(g, c)][:])
+
+        def quantise_y(g, c):
+            quantise(("y", g, c), y_codes[(g, c)][:], y_plane[:, g, group(c)])
+
+        def second_product(g, c, order):
+            acc = take_banks(("z", g, c))
+            for s, u in order:
+                cols = slice(P * s, P * (s + 1))
+                nc.tensor.matmul_mx(
+                    out=acc[s][:],
+                    lhsT=f_codes[(g, u)][:, cols].bitcast(FP8X4),
+                    lhsT_scale=f_plane[(g, u)][:, cols],
+                    rhs=ket_codes[(u, c)][:].bitcast(FP8X4),
+                    rhs_scale=ket_plane[(u, c)][:],
+                    start=(u == 0),
+                    stop=(u == S - 1),
+                )
+
+        pass_by_pass = [(s, u) for u in range(S) for s in range(PACK)]
+        bank_by_bank = [(s, u) for s in range(PACK) for u in range(S)]
+
+        def row_factor(g, s):
+            return scale_col[:, PACK * g + s : PACK * g + s + 1]
+
+        def scale_local_on_scalar(g, c, slots):
+            for s in slots:
+                nc.scalar.activation(
+                    out=y_rows[(g, c)][:, s, :], in_=local_rows[g][:, s, group(c)], func=COPY, scale=row_factor(g, s)
+                )
+
+        def scale_local_on_vector(g, c, slots):
+            for s in slots:
+                nc.vector.tensor_scalar(
+                    out=y_rows[(g, c)][:, s, :],
+                    in0=local_rows[g][:, s, group(c)],
+                    scalar1=row_factor(g, s),
+                    scalar2=None,
+                    op0=ALU.mult,
+                )
+
+        def finish(g, c):
+            for s in range(PACK):
+                nc.vector.scalar_tensor_tensor(
+                    out=y_rows[(g, c)][:, s, :],
+                    in0=banks[("z", g, c)][s][:],
+                    scalar=row_factor(g, s),
+                    in1=y_rows[(g, c)][:, s, :],
+                    op0=ALU.mult,
+                    op1=ALU.add,
+                )
+
+        def store_y(g, c):
+            for slots in (slice(0, 2), slice(2, PACK)):
+                nc.sync.dma_start(out=by_slot(out_0[group(g), group(c)])[:, slots, :], in_=y_rows[(g, c)][:, slots, :])
+
+        def store_codes(g, c):
+            words = out_1[g, :, group(c), :].rearrange("p m t -> p (m t)")
+            nc.sync.dma_start(out=words.bitcast(I32), in_=y_codes[(g, c)][:].bitcast(I32))
+
+        def store_plane():
+            for q in range(4):
+                rows = out_2[:, 4 * q : 4 * q + 4, :].rearrange("g r n -> r g n")
+                nc.sync.dma_start(out=rows.bitcast(I32), in_=y_plane[32 * q : 32 * q + 4].bitcast(I32))
+
+        on_vector, on_scalar = nc.vector.tensor_copy, nc.scalar.copy
+        every_slot = range(PACK)
+
+        zero_plane(env_raw_plane)
+        zero_plane(bra_plane[0])
+        ones = keep("ones", [P, GROUP], BF16)
+        ones_codes = keep("ones_codes", [P, P], U32)
+        ones_plane = keep("ones_plane", [P, P], U8)
+        nc.vector.memset(ones[:], 1.0)
+        nc.vector.quantize_mx(out=ones_codes[:].bitcast(FP8X4), scales=ones_plane[:], in_=ones[:])
+        spare = psum.tile([P, PACK, P], F32, name="bank7")
+        for n in range(WARM_PASSES):
+            nc.tensor.matmul_mx(
+                out=spare[:, n % PACK, :],
+                lhsT=ones_codes[:].bitcast(FP8X4),
+                lhsT_scale=ones_plane[:],
+                rhs=ones_codes[:].bitcast(FP8X4),
+                rhs_scale=ones_plane[:],
+                start=True,
+                stop=True,
+            )
+        zero_plane(bra_plane[RB])
+        zero_plane(bra_plane[2 * RB])
+        load_words(env_raw, env_words, 0, LK)
+        load_plane(env_raw_plane, env_scales, 0, LK)
+        load_bra(0)
+        load_bra(1)
+        load_bra_plane(0)
+        load(weight_raw[:].rearrange("p (u t) -> p u t", t=PACK), weight.rearrange("u (p t) -> p u t", t=PACK))
+        load_ket(0, 0)
+        load_bra(2)
+        load_ket(0, 1)
+        load_bra_plane(1)
+        load_bra(3)
+        load_ket(1, 0)
+        load_bra_plane(2)
+        load_ket(2, 0)
+        load_bra(4)
+        load(scale_raw[:].rearrange("p (g s) -> p g s", s=PACK), row_scale.rearrange("(g p s) -> p g s", p=P, s=PACK))
+        load_ket(3, 0)
+        for g in range(HALVES):
+            load(local_rows[g][:], by_slot(local[group(g), :]))
 
         for t in range(PACK):
-            env_perm(t)
+            slice_env(t)
+        nc.scalar.activation(out=weight_col[:], in_=weight_raw[:], func=COPY)
 
-        def first(g, u, t):
-            bank = PACK * (pe_units.index("S1_%d%d" % (g, u)) % 2) + t
-            if u == 0:
-                words, wcols, wload = bra_w[(g, u)], slice(0, 2 * BANK), ("ld", "bra", g, 0)
-            else:
-                words, wcols, wload = bra_wu[u], slice(2 * BANK * g, 2 * BANK * (g + 1)), ("ld", "brau", u)
-            plane, s0, sname = bra_s[u], BANK * g, "bra_s%d" % u
+        first_product(0, 0)
+        weigh(0, 0)
+        mix_ket(on_vector, 0, 0)
+        quantise_ket(0, 0)
+        first_product(1, 0)
+        weigh(1, 0)
+        mix_f(on_vector, 0, 0)
+        mix_ket(on_vector, 0, 1)
+        quantise_f(0, 0)
+        first_product(0, 1)
+        weigh(0, 1)
+        mix_f(on_vector, 1, 0)
+        quantise_ket(0, 1)
+        first_product(1, 1)
+        weigh(1, 1)
+        mix_ket(on_vector, 1, 0)
+        quantise_f(1, 0)
+        mix_f(on_vector, 0, 1)
+        quantise_ket(1, 0)
+        first_product(0, 2)
+        weigh(0, 2)
+        mix_ket(on_vector, 2, 0)
+        mix_f(on_scalar, 1, 1)
+        quantise_f(0, 1)
+        mix_f(on_vector, 0, 2)
+        quantise_ket(2, 0)
+        first_product(0, 3)
+        weigh(0, 3)
+        mix_ket(on_vector, 3, 0)
+        quantise_f(0, 2)
+        quantise_f(1, 1)
+        first_product(1, 2)
+        weigh(1, 2)
+        mix_f(on_vector, 0, 3)
+        quantise_ket(3, 0)
+        first_product(1, 3)
+        weigh(1, 3)
+        mix_ket(on_vector, 2, 1)
+        quantise_f(0, 3)
 
-            def mm(e):
-                acc = fresh("bank%d" % bank, psum, [P, BANK], F32, ("H", g, u, t))
-                for h in range(2):
-                    nc.tensor.matmul_mx(
-                        out=acc[:], lhsT=env_w[t][:, h, :].bitcast(FP4X4), lhsT_scale=env_s[t][:, h, :],
-                        rhs=words[:, h, wcols].bitcast(FP4X4), rhs_scale=plane[:, h, s0 : s0 + BANK],
-                        start=(h == 0), stop=(h == 1))
-
-            job(("S1", g, u, t), [("envw", t), ("envs", t), wload] + [("ld", sname, q) for q in range(4)], mm,
-                slot="bank%d" % bank)
-            job(("E1", g, u, t), [("S1", g, u, t), ("w32",)], lambda e: nc.scalar.activation(
-                out=f_raw[(g, u)][:, t, :].rearrange("p (s m) -> p s m", s=PACK),
-                in_=live[("H", g, u, t)][:].rearrange("p (m s) -> p s m", s=PACK),
-                func=COPY, scale=w32[:, PACK * u + t : PACK * u + t + 1]), frees="bank%d" % bank)
-
-        for (g, u) in FIRST_ORDER:
-            for t in range(PACK):
-                first(g, u, t)
-
-        def quant(kind, key, needs, src, width, codes, scales, slot):
-            tag = "wide%d" % slot
-            job((kind + "I",) + key, needs,
-                lambda e: interleave(e, fresh(tag, sb, [P, PACK * width], BF16, (kind,) + key)[:], src), slot=tag)
-            job((kind + "Q",) + key, [(kind + "I",) + key], lambda e: nc.vector.quantize_mx(
-                out=codes.bitcast(FP8X4), scales=scales, in_=live[(kind,) + key][:]), frees=tag)
-
-        def second(n, g, j0, w, s):
-            bank = PACK * ([w[1:] for w in pe_units].index(str(n)) % 2) + s
-            jh, c0 = divmod(j0, BANK)
-
-            def mm(u):
-                def run(e):
-                    if u == 0:
-                        fresh("bank%d" % bank, psum, [P, BANK], F32, ("Z", n, s))
-                    nc.tensor.matmul_mx(
-                        out=live[("Z", n, s)][:, 0:w],
-                        lhsT=f_c[(g, u)][:, P * s : P * (s + 1)].bitcast(FP8X4),
-                        lhsT_scale=f_s[(g, u)][:, P * s : P * (s + 1)],
-                        rhs=ket_c[(u, jh)][:, c0 : c0 + w].bitcast(FP8X4), rhs_scale=ket_s[(u, jh)][:, c0 : c0 + w],
-                        start=(u == 0), stop=(u == S - 1))
-                return run
-
-            for u in range(S):
-                job(("S2", n, s, u), [("FQ", g, u), ("KQ", u, jh)] + ([("S2", n, s, u - 1)] if u else []), mm(u),
-                    slot="bank%d" % bank if u == 0 else None)
-            col = rs32[:, PACK * g + s : PACK * g + s + 1]
-            tag = "lrs%d" % (s if on_gpsimd else PACK * (n % 2) + s)
-
-            def lrs(e):
-                dst = fresh(tag, sb, [P, w], F32, ("L", n, s))
-                if e == "S":
-                    nc.scalar.activation(out=dst[:], in_=loc[g][:, s, j0 : j0 + w], func=COPY, scale=col)
-                elif e == "G":
-                    nc.gpsimd.tensor_scalar(out=dst[:], in0=loc[g][:, s, j0 : j0 + w], scalar1=col, scalar2=0.0,
-                                            op0=ALU.mult, op1=ALU.add)
-                else:
-                    nc.vector.tensor_scalar(out=dst[:], in0=loc[g][:, s, j0 : j0 + w], scalar1=col, scalar2=None, op0=ALU.mult)
-
-            job(("LRS", n, s), [("ld", "loc", g), ("rs32",)] + ([("E2", n - 1, s)] if on_gpsimd and n else []), lrs, slot=tag)
-            job(("E2", n, s), [("S2", n, s, S - 1), ("LRS", n, s)], lambda e: nc.vector.scalar_tensor_tensor(
-                out=y32[n][:, s, :], in0=live[("Z", n, s)][:, 0:w], scalar=col, in1=live[("L", n, s)][:],
-                op0=ALU.mult, op1=ALU.add), frees=("bank%d" % bank, tag))
-
-        for n, (g, j0, w) in enumerate(OUT_UNITS):
-            for s in range(PACK):
-                second(n, g, j0, w, s)
-
-        def store_rows(n, g, j0, w, s0, ns):
-            rows = out_0[KP * g : KP * (g + 1), j0 : j0 + w].rearrange("(p t) j -> p t j", t=PACK)
-            job(("st", "y", n, s0), [("E2", n, s) for s in range(s0, s0 + ns)], lambda e: queue[e].dma_start(
-                out=rows[:, s0 : s0 + ns, :], in_=y32[n][:, s0 : s0 + ns, :]))
-
-        def store_codes(g, jh):
-            job(("st", "c", g, jh), [("YQ", n) for n, x in enumerate(OUT_UNITS) if x[0] == g and x[1] // BANK == jh],
-                lambda e: queue[e].dma_start(
-                    out=out_1[g, :, BANK * jh : BANK * (jh + 1), :].rearrange("p m t -> p (m t)").bitcast(I32),
-                    in_=y_c[(g, jh)][:].bitcast(I32)))
-
-        def store_scales(g, q):
-            job(("st", "s", g, q), [("YQ", n) for n, x in enumerate(OUT_UNITS) if x[0] == g],
-                lambda e: queue[e].dma_start(out=out_2[g, 4 * q : 4 * q + 4, :].bitcast(I32),
-                                             in_=y_s[g][32 * q : 32 * q + 4, :].bitcast(I32)))
-
-        for n, (g, j0, w) in enumerate(OUT_UNITS):
-            for s0 in (0, 2):
-                store_rows(n, g, j0, w, s0, 2)
-        for g in range(2):
-            for q in range(4):
-                store_scales(g, q)
-            for jh in range(2):
-                store_codes(g, jh)
-
-        def unit(kind, *key):
-            return [(kind,) + key + (s,) for s in range(PACK)]
-
-        def expand(word):
-            d = tuple(int(c) for c in word.split("_")[-1] if c in "0123456789")
-            kind = "".join(c for c in word if c not in "0123456789")
-            if word[:2] in ("S1", "E1", "E2"):
-                d = tuple(int(c) for c in word[3:])
-                kind = word[:3]
-            if kind == "b":
-                return [("S2", d[0], s, u) for s in range(PACK) for u in range(S)]
-            if kind == "p":
-                return [("S2", d[0], s, u) for u in range(S) for s in range(PACK)]
-            if kind in ("S1_", "E1_", "E2_", "LRS_"):
-                return unit(kind[:-1], *d)
-            if kind in ("E2h", "LRSh"):
-                return [(kind[:-1], d[0], 2 * d[1]), (kind[:-1], d[0], 2 * d[1] + 1)]
-            if kind == "env":
-                return [("envw", d[0]), ("envs", d[0])]
-            if word in ("w32", "rs32"):
-                return [(word,)]
-            if word == "Z":
-                return [("zero", "env_s")] + [("zero", "bra_s%d" % u) for u in range(S)]
-            if word == "le":
-                return [("ld", "env")]
-            if word == "les":
-                return unit("ld", "env_s")
-            if kind == "lbs":
-                return unit("ld", "bra_s%d" % d[0])
-            if word in ("lw", "lrs"):
-                return [("ld", word[1:])]
-            if kind == "lb":
-                return [("ld", "bra") + d] if len(d) == 2 else [("ld", "brau") + d]
-            if kind == "lk":
-                return [("ld", "ket") + d]
-            if kind == "ll":
-                return [("ld", "loc") + d]
-            if kind == "sy":
-                return [("st", "y", d[0], 0), ("st", "y", d[0], 2)]
-            if kind == "sc":
-                return [("st", "c") + d]
-            if kind == "ss":
-                return unit("st", "s", *d)
-            return [(kind,) + d]
-
-        order = {e: [j for word in ORDER[e].split() for j in expand(word)] for e in ORDER}
-
-        quantised = [j for j in order["V"] if j[0] in ("KQ", "FQ", "YQ")]
-        for n, j in enumerate(quantised):
-            key = j[1:]
-            if j[0] == "KQ":
-                u, jh = key
-                if u == 0:
-                    need, src = ("ld", "ket", 0, jh), ket_first[jh][:]
-                else:
-                    need, src = ("ld", "ket", u), ket_rest[u][:, :, BANK * jh : BANK * (jh + 1)]
-                quant("K", key, [need], src, BANK, ket_c[key][:], ket_s[key][:], n % WIDE)
-            elif j[0] == "FQ":
-                quant("F", key, unit("E1", *key), f_raw[key][:], KP, f_c[key][:], f_s[key][:], n % WIDE)
-            else:
-                g, j0, w = OUT_UNITS[key[0]]
-                jh, c0 = divmod(j0, BANK)
-                quant("Y", key, unit("E2", *key), y32[key[0]][:], w, y_c[(g, jh)][:, c0 : c0 + w],
-                      y_s[g][:, j0 : j0 + w], n % WIDE)
-
-        assert sorted(map(str, jobs)) == sorted(str(j) for e in order for j in order[e])
-        done = set()
-        taken = set()
-        at = {e: 0 for e in order}
-        for sweep in range(len(jobs)):
-            for e in order:
-                if at[e] < len(order[e]):
-                    name = order[e][at[e]]
-                    needs, run, slot, frees = jobs[name]
-                    if all(d in done for d in needs) and slot not in taken:
-                        run(e)
-                        done.add(name)
-                        at[e] += 1
-                        if slot is not None:
-                            taken.add(slot)
-                        if frees is not None:
-                            for f in (frees if isinstance(frees, tuple) else (frees,)):
-                                taken.remove(f)
-        assert len(done) == len(jobs)
+        second_product(0, 0, pass_by_pass)
+        mix_f(on_vector, 1, 2)
+        nc.scalar.activation(out=scale_col[:], in_=scale_raw[:], func=COPY)
+        mix_ket(on_scalar, 1, 1)
+        quantise_ket(2, 1)
+        mix_f(on_vector, 1, 3)
+        scale_local_on_scalar(0, 0, every_slot)
+        quantise_f(1, 2)
+        quantise_ket(1, 1)
+        quantise_f(1, 3)
+        second_product(1, 0, pass_by_pass)
+        finish(0, 0)
+        store_y(0, 0)
+        mix_ket(on_scalar, 3, 1)
+        scale_local_on_vector(0, 1, every_slot)
+        scale_local_on_scalar(1, 0, every_slot)
+        quantise_ket(3, 1)
+        second_product(0, 1, pass_by_pass)
+        finish(1, 0)
+        store_y(1, 0)
+        mix_y(on_scalar, 0, 0)
+        second_product(1, 1, bank_by_bank)
+        finish(0, 1)
+        store_y(0, 1)
+        scale_local_on_scalar(1, 1, every_slot[2:])
+        mix_y(on_scalar, 1, 0)
+        quantise_y(0, 0)
+        store_codes(0, 0)
+        scale_local_on_vector(1, 1, every_slot[:2])
+        finish(1, 1)
+        store_y(1, 1)
+        mix_y(on_scalar, 0, 1)
+        quantise_y(1, 0)
+        store_codes(1, 0)
+        mix_y(on_vector, 1, 1)
+        quantise_y(0, 1)
+        quantise_y(1, 1)
+        store_codes(0, 1)
+        store_codes(1, 1)
+        store_plane()

@@ -25,7 +25,6 @@ BRA_PIECES = [(0, GROUP), (GROUP, GROUP), (RB, RB), (2 * RB, RB), (3 * RB, RB)]
 BRA_PLANE_PIECES = [(0, RB), (RB, RB), (2 * RB, 2 * RB)]
 KET_PIECES = {0: [(0, GROUP), (GROUP, GROUP)], 1: [(0, RK)], 2: [(0, RK)], 3: [(0, RK)]}
 STAGING = 6
-WARM_PASSES = 30
 
 
 def tile_site_environment_absorption_k5_kernel(
@@ -241,22 +240,6 @@ def tile_site_environment_absorption_k5_kernel(
 
         zero_plane(env_raw_plane)
         zero_plane(bra_plane[0])
-        ones = keep("ones", [P, GROUP], BF16)
-        ones_codes = keep("ones_codes", [P, P], U32)
-        ones_plane = keep("ones_plane", [P, P], U8)
-        nc.vector.memset(ones[:], 1.0)
-        nc.vector.quantize_mx(out=ones_codes[:].bitcast(FP8X4), scales=ones_plane[:], in_=ones[:])
-        spare = psum.tile([P, PACK, P], F32, name="bank7")
-        for n in range(WARM_PASSES):
-            nc.tensor.matmul_mx(
-                out=spare[:, n % PACK, :],
-                lhsT=ones_codes[:].bitcast(FP8X4),
-                lhsT_scale=ones_plane[:],
-                rhs=ones_codes[:].bitcast(FP8X4),
-                rhs_scale=ones_plane[:],
-                start=True,
-                stop=True,
-            )
         zero_plane(bra_plane[RB])
         zero_plane(bra_plane[2 * RB])
         load_words(env_raw, env_words, 0, LK)

from contextlib import ExitStack

import concourse.mybir as mybir

S, LB, LK, RB, RK = 4, 1024, 512, 1024, 1024
FLOPS = 2 * LB * S * RB * LK + 2 * RB * S * LK * RK

F32 = mybir.dt.float32
BF16 = mybir.dt.bfloat16
I32 = mybir.dt.int32
U32 = mybir.dt.uint32
U8 = mybir.dt.uint8
FP8X4 = mybir.dt.float8_e4m3fn_x4
FP4X4 = mybir.dt.float4_e2m1fn_x4
ALU = mybir.AluOpType
COPY = mybir.ActivationFunctionType.Copy

P = 128
PACK = 4
GROUP = P * PACK
PASSES = LB // GROUP
HALVES = 2
RUN = 4
BRA_PIECES = [(0, GROUP), (GROUP, GROUP), (RB, RB), (2 * RB, RB), (3 * RB, RB)]
BRA_PLANE_PIECES = [(0, RB), (RB, RB), (2 * RB, 2 * RB)]
KET_PIECES = {0: [(0, GROUP), (GROUP, GROUP)], 1: [(0, RK)], 2: [(0, RK)], 3: [(0, RK)]}
STAGING = 6


def tile_site_environment_absorption_k5_kernel(
    tc, bra_words, bra_scales, env_words, env_scales, weight, ket, local, row_scale, out_0, out_1, out_2
):
    nc = tc.nc
    with ExitStack() as ctx:
        sbuf = ctx.enter_context(tc.tile_pool(name="sbuf", bufs=1))
        psum = ctx.enter_context(tc.psum_pool(name="psum", bufs=1))
        ctx.enter_context(tc.manual_schedule())

        def keep(name, shape, dtype):
            return sbuf.tile(shape, dtype, name=name, align_bytes=64)

        sites = [(g, u) for g in range(HALVES) for u in range(S)]
        kets = [(u, c) for u in range(S) for c in range(HALVES)]
        blocks = [(g, c) for g in range(HALVES) for c in range(HALVES)]

        env_raw = keep("env_raw", [P, PASSES, 2 * LK], U8)
        env_raw_plane = keep("env_raw_plane", [P, PASSES, LK], U8)
        env_slice = [keep("env_slice%d" % t, [P, PASSES, 2 * P], U8) for t in range(PACK)]
        env_slice_plane = [keep("env_slice_plane%d" % t, [P, PASSES, P], U8) for t in range(PACK)]
        bra = {first: keep("bra%d" % first, [P, PASSES, 2 * cols], U8) for first, cols in BRA_PIECES}
        bra_plane = {first: keep("bra_plane%d" % first, [P, PASSES, cols], U8) for first, cols in BRA_PLANE_PIECES}
        weight_raw = keep("weight_raw", [P, S * PACK], BF16)
        weight_col = keep("weight_col", [P, S * PACK], F32)
        scale_raw = keep("scale_raw", [P, HALVES * PACK], BF16)
        scale_col = keep("scale_col", [P, HALVES * PACK], F32)
        ket_rows = {
            u: {first: keep("ket_rows%d_%d" % (u, first), [P, PACK, cols], BF16) for first, cols in KET_PIECES[u]}
            for u in range(S)
        }
        local_rows = [keep("local_rows%d" % g, [P, PACK, RK], BF16) for g in range(HALVES)]
        f_rows = {site: keep("f_rows%d%d" % site, [P, PACK, GROUP], BF16) for site in sites}
        y_rows = {block: keep("y_rows%d%d" % block, [P, PACK, GROUP], F32) for block in blocks}
        ket_codes = {k: keep("ket_codes%d%d" % k, [P, GROUP], U32) for k in kets}
        ket_plane = {k: keep("ket_plane%d%d" % k, [P, GROUP], U8) for k in kets}
        f_codes = {site: keep("f_codes%d%d" % site, [P, GROUP], U32) for site in sites}
        f_plane = {site: keep("f_plane%d%d" % site, [P, GROUP], U8) for site in sites}
        y_codes = {block: keep("y_codes%d%d" % block, [P, GROUP], U32) for block in blocks}
        y_plane = keep("y_plane", [P, HALVES, RK], U8)

        banks = {}
        staged = {}

        def group(n):
            return slice(GROUP * n, GROUP * (n + 1))

        def by_slot(rows):
            return rows.rearrange("(p t) j -> p t j", t=PACK)

        def window(pieces, first, bytes_a_column=1):
            start = max(n for n in pieces if n <= first)
            return pieces[start][:, :, bytes_a_column * (first - start) : bytes_a_column * (first - start + GROUP)]

        def load(dst, src):
            nc.sync.dma_start(out=dst, in_=src)

        def load_words(dst, words, first, cols):
            src = words.rearrange("h p n -> p h n")[:, :, 2 * first : 2 * (first + cols)]
            load(dst[:].bitcast(I32), src.bitcast(I32))

        def load_plane(plane, scales, first, cols):
            for q in range(4):
                rows = scales[:, 4 * q : 4 * q + 4, first : first + cols].rearrange("h r n -> r h n")
                load(plane[32 * q : 32 * q + 4].bitcast(I32), rows.bitcast(I32))

        def zero_plane(plane):
            nc.vector.memset(plane[:].bitcast(I32), 0)

        def load_bra(n):
            first, cols = BRA_PIECES[n]
            load_words(bra[first], bra_words, first, cols)

        def load_bra_plane(n):
            first, cols = BRA_PLANE_PIECES[n]
            load_plane(bra_plane[first], bra_scales, first, cols)

        def load_ket(u, n):
            first, cols = KET_PIECES[u][n]
            load(ket_rows[u][first][:], by_slot(ket[group(u), first : first + cols]))

        def slice_env(t):
            nc.vector.tensor_copy(
                out=env_slice[t][:].rearrange("p h (m b) -> p h m b", b=2),
                in_=env_raw[:].rearrange("p h (m t b) -> p t h m b", t=PACK, b=2)[:, t],
            )
            nc.vector.tensor_copy(
                out=env_slice_plane[t][:], in_=env_raw_plane[:].rearrange("p h (m t) -> p t h m", t=PACK)[:, t]
            )

        def take_banks(product):
            first = PACK * (len(banks) % 2)
            banks[product] = [psum.tile([P, GROUP], F32, name="bank%d" % (first + t)) for t in range(PACK)]
            return banks[product]

        def first_product(g, u):
            acc = take_banks(("h", g, u))
            words = window(bra, RB * u + GROUP * g, bytes_a_column=2)
            plane = window(bra_plane, RB * u + GROUP * g)
            for t in range(PACK):
                for h in range(PASSES):
                    nc.tensor.matmul_mx(
                        out=acc[t][:],
                        lhsT=env_slice[t][:, h, :].bitcast(FP4X4),
                        lhsT_scale=env_slice_plane[t][:, h, :],
                        rhs=words[:, h, :].bitcast(FP4X4),
                        rhs_scale=plane[:, h, :],
                        start=(h == 0),
                        stop=(h == PASSES - 1),
                    )

        def weigh(g, u):
            for t in range(PACK):
                nc.scalar.activation(
                    out=f_rows[(g, u)][:, t, :].rearrange("p (s m) -> p s m", s=PACK),
                    in_=banks[("h", g, u)][t][:].rearrange("p (m s) -> p s m", s=PACK),
                    func=COPY,
                    scale=weight_col[:, PACK * u + t : PACK * u + t + 1],
                )

        def interleave(copy, operand, rows):
            tile = keep("staging%d" % (len(staged) % STAGING), [P, PACK * GROUP], BF16)
            staged[operand] = tile
            copy(
                out=tile[:].rearrange("p (n i t) -> p n t i", i=RUN, t=PACK),
                in_=rows.rearrange("p t (n i) -> p n t i", i=RUN),
            )

        def quantise(operand, codes, plane):
            nc.vector.quantize_mx(out=codes.bitcast(FP8X4), scales=plane, in_=staged[operand][:])

        def mix_ket(copy, u, c):
            interleave(copy, ("ket", u, c), window(ket_rows[u], GROUP * c))

        def quantise_ket(u, c):
            quantise(("ket", u, c), ket_codes[(u, c)][:], ket_plane[(u, c)][:])

        def mix_f(copy, g, u):
            interleave(copy, ("f", g, u), f_rows[(g, u)][:])

        def quantise_f(g, u):
            quantise(("f", g, u), f_codes[(g, u)][:], f_plane[(g, u)][:])

        def mix_y(copy, g, c):
            interleave(copy, ("y", g, c), y_rows[(g, c)][:])

        def quantise_y(g, c):
            quantise(("y", g, c), y_codes[(g, c)][:], y_plane[:, g, group(c)])

        def second_product(g, c, order):
            acc = take_banks(("z", g, c))
            for s, u in order:
                cols = slice(P * s, P * (s + 1))
                nc.tensor.matmul_mx(
                    out=acc[s][:],
                    lhsT=f_codes[(g, u)][:, cols].bitcast(FP8X4),
                    lhsT_scale=f_plane[(g, u)][:, cols],
                    rhs=ket_codes[(u, c)][:].bitcast(FP8X4),
                    rhs_scale=ket_plane[(u, c)][:],
                    start=(u == 0),
                    stop=(u == S - 1),
                )

        pass_by_pass = [(s, u) for u in range(S) for s in range(PACK)]
        bank_by_bank = [(s, u) for s in range(PACK) for u in range(S)]

        def row_factor(g, s):
            return scale_col[:, PACK * g + s : PACK * g + s + 1]

        def scale_local_on_scalar(g, c, slots):
            for s in slots:
                nc.scalar.activation(
                    out=y_rows[(g, c)][:, s, :], in_=local_rows[g][:, s, group(c)], func=COPY, scale=row_factor(g, s)
                )

        def scale_local_on_vector(g, c, slots):
            for s in slots:
                nc.vector.tensor_scalar(
                    out=y_rows[(g, c)][:, s, :],
                    in0=local_rows[g][:, s, group(c)],
                    scalar1=row_factor(g, s),
                    scalar2=None,
                    op0=ALU.mult,
                )

        def finish(g, c):
            for s in range(PACK):
                nc.vector.scalar_tensor_tensor(
                    out=y_rows[(g, c)][:, s, :],
                    in0=banks[("z", g, c)][s][:],
                    scalar=row_factor(g, s),
                    in1=y_rows[(g, c)][:, s, :],
                    op0=ALU.mult,
                    op1=ALU.add,
                )

        def store_y(g, c):
            for slots in (slice(0, 2), slice(2, PACK)):
                nc.sync.dma_start(out=by_slot(out_0[group(g), group(c)])[:, slots, :], in_=y_rows[(g, c)][:, slots, :])

        def store_codes(g, c):
            words = out_1[g, :, group(c), :].rearrange("p m t -> p (m t)")
            nc.sync.dma_start(out=words.bitcast(I32), in_=y_codes[(g, c)][:].bitcast(I32))

        def store_plane():
            for q in range(4):
                rows = out_2[:, 4 * q : 4 * q + 4, :].rearrange("g r n -> r g n")
                nc.sync.dma_start(out=rows.bitcast(I32), in_=y_plane[32 * q : 32 * q + 4].bitcast(I32))

        on_vector, on_scalar = nc.vector.tensor_copy, nc.scalar.copy
        every_slot = range(PACK)

        zero_plane(env_raw_plane)
        zero_plane(bra_plane[0])
        zero_plane(bra_plane[RB])
        zero_plane(bra_plane[2 * RB])
        load_words(env_raw, env_words, 0, LK)
        load_plane(env_raw_plane, env_scales, 0, LK)
        load_bra(0)
        load_bra(1)
        load_bra_plane(0)
        load(weight_raw[:].rearrange("p (u t) -> p u t", t=PACK), weight.rearrange("u (p t) -> p u t", t=PACK))
        load_ket(0, 0)
        load_bra(2)
        load_ket(0, 1)
        load_bra_plane(1)
        load_bra(3)
        load_ket(1, 0)
        load_bra_plane(2)
        load_ket(2, 0)
        load_bra(4)
        load(scale_raw[:].rearrange("p (g s) -> p g s", s=PACK), row_scale.rearrange("(g p s) -> p g s", p=P, s=PACK))
        load_ket(3, 0)
        for g in range(HALVES):
            load(local_rows[g][:], by_slot(local[group(g), :]))

        for t in range(PACK):
            slice_env(t)
        nc.scalar.activation(out=weight_col[:], in_=weight_raw[:], func=COPY)

        first_product(0, 0)
        weigh(0, 0)
        mix_ket(on_vector, 0, 0)
        quantise_ket(0, 0)
        first_product(1, 0)
        weigh(1, 0)
        mix_f(on_vector, 0, 0)
        mix_ket(on_vector, 0, 1)
        quantise_f(0, 0)
        first_product(0, 1)
        weigh(0, 1)
        mix_f(on_vector, 1, 0)
        quantise_ket(0, 1)
        first_product(1, 1)
        weigh(1, 1)
        mix_ket(on_vector, 1, 0)
        quantise_f(1, 0)
        mix_f(on_vector, 0, 1)
        quantise_ket(1, 0)
        first_product(0, 2)
        weigh(0, 2)
        mix_ket(on_vector, 2, 0)
        mix_f(on_scalar, 1, 1)
        quantise_f(0, 1)
        mix_f(on_vector, 0, 2)
        quantise_ket(2, 0)
        first_product(0, 3)
        weigh(0, 3)
        mix_ket(on_vector, 3, 0)
        quantise_f(0, 2)
        quantise_f(1, 1)
        first_product(1, 2)
        weigh(1, 2)
        mix_f(on_vector, 0, 3)
        quantise_ket(3, 0)
        first_product(1, 3)
        weigh(1, 3)
        mix_ket(on_vector, 2, 1)
        quantise_f(0, 3)

        second_product(0, 0, pass_by_pass)
        mix_f(on_vector, 1, 2)
        nc.scalar.activation(out=scale_col[:], in_=scale_raw[:], func=COPY)
        mix_ket(on_scalar, 1, 1)
        quantise_ket(2, 1)
        mix_f(on_vector, 1, 3)
        scale_local_on_scalar(0, 0, every_slot)
        quantise_f(1, 2)
        quantise_ket(1, 1)
        quantise_f(1, 3)
        second_product(1, 0, pass_by_pass)
        finish(0, 0)
        store_y(0, 0)
        mix_ket(on_scalar, 3, 1)
        scale_local_on_vector(0, 1, every_slot)
        scale_local_on_scalar(1, 0, every_slot)
        quantise_ket(3, 1)
        second_product(0, 1, pass_by_pass)
        finish(1, 0)
        store_y(1, 0)
        mix_y(on_scalar, 0, 0)
        second_product(1, 1, bank_by_bank)
        finish(0, 1)
        store_y(0, 1)
        scale_local_on_scalar(1, 1, every_slot[2:])
        mix_y(on_scalar, 1, 0)
        quantise_y(0, 0)
        store_codes(0, 0)
        scale_local_on_vector(1, 1, every_slot[:2])
        finish(1, 1)
        store_y(1, 1)
        mix_y(on_scalar, 0, 1)
        quantise_y(1, 0)
        store_codes(1, 0)
        mix_y(on_vector, 1, 1)
        quantise_y(0, 1)
        quantise_y(1, 1)
        store_codes(0, 1)
        store_codes(1, 1)
        store_plane()
